import numpy as np
import ml_dtypes


def mxq(x, axis, fmt="e4m3"):
    dtype, down = {"e4m3": (ml_dtypes.float8_e4m3fn, 7), "e5m2": (ml_dtypes.float8_e5m2, 14)}[fmt]
    v = np.moveaxis(np.asarray(x, np.float32).astype(ml_dtypes.bfloat16).astype(np.float64), axis, -1)
    blocks = v.reshape(v.shape[:-1] + (-1, 32))
    amax = np.abs(blocks).max(-1, keepdims=True)
    byte = np.maximum(np.where(amax > 0, np.frexp(amax)[1] - 1 + 127, 0) - down, 1)
    scale = np.exp2(byte - 127.0)
    codes = (blocks / scale).astype(np.float32).astype(dtype).astype(np.float64)
    return np.moveaxis((codes * scale).reshape(v.shape), -1, axis)


WIDE = False


def mx_kscale(k):
    if not WIDE:
        return np.ones(k)
    levels = np.array([30, -30])
    if k % 512:
        return np.exp2(np.random.permutation(np.resize(levels, k // 32))).repeat(32)
    a = np.empty((k // 512, 16))
    for p in range(k // 512):
        a[p, :8] = np.random.permutation(np.resize(levels, 8))
        for g in range(8):
            far = levels[np.abs(levels - a[p, g]) >= 10]
            a[p, g + 8] = far[np.random.randint(len(far))]
    return np.exp2(a.ravel()).repeat(32)


def f64(x):
    return np.asarray(x).astype(np.float64)


def striped(idx):
    return np.tile(idx.reshape(-1, 16).T, (8, 1)).astype(np.uint16)


def unstriped(offs):
    return offs[:16].T.reshape(-1).astype(np.int64)


E2M1 = np.array([0.0, 0.5, 1.0, 1.5, 2.0, 3.0, 4.0, 6.0, -0.0, -0.5, -1.0, -1.5, -2.0, -3.0, -4.0, -6.0])


def pack_weight(w, fmt):
    k, n = w.shape
    w = f64(np.asarray(w, np.float32).astype(ml_dtypes.bfloat16)).reshape(k // 32, 32, n)
    amax = np.abs(w).max(1)
    if fmt == "e4m3":
        byte = np.frexp(amax)[1] - 1 + 127 - 7
    else:
        mant, ex = np.frexp(amax / 6.0)
        byte = np.where(mant > 0.5, ex, ex - 1) + 127
    byte = np.clip(np.where(amax > 0, byte, 1), 1, 254)
    scaled = (w * np.exp2(127.0 - byte)[:, None, :]).reshape(k, n).astype(np.float32)
    by_word = np.ascontiguousarray(scaled.reshape(k // 512, 128, 4, n).transpose(0, 1, 3, 2))
    if fmt == "e4m3":
        words = by_word.astype(ml_dtypes.float8_e4m3fn).view(np.uint8)
    else:
        c = by_word.astype(ml_dtypes.float4_e2m1fn).view(np.uint8) & 0xF
        words = (c[..., 0::2] | (c[..., 1::2] << 4)).reshape(k // 512, 128, 2 * n)
    return np.ascontiguousarray(words), np.ascontiguousarray(byte.astype(np.uint8).reshape(k // 512, 16, n))


def unpack_weight(words, scales, fmt):
    g, _, n = scales.shape
    words = np.ascontiguousarray(words).reshape(g, 128, n, -1)
    if fmt == "e4m3":
        vals = words.view(ml_dtypes.float8_e4m3fn).astype(np.float64)
    else:
        nib = np.empty((g, 128, n, 4), np.uint8)
        nib[..., 0::2] = words & 0xF
        nib[..., 1::2] = words >> 4
        vals = E2M1[nib]
    vals = vals * np.repeat(np.exp2(scales.astype(np.float64) - 127.0), 8, axis=1)[..., None]
    return vals.transpose(0, 1, 3, 2).reshape(g * 512, n)


def d_relu(v):
    return (v > 0).astype(np.float64)


K, T, E, C, H, N = 128, 1024, 4, 512, 512, 512


def by_expert(wq, xq):
    return np.concatenate([wq[e].T @ xq[:, e * C:(e + 1) * C] for e in range(E)], axis=1)


def setup_inputs():
    n = np.random.standard_normal
    s = mx_kscale(N)[:, None]
    u = mx_kscale(H)
    first = np.random.permutation(np.repeat(np.arange(E), T // E))
    second = (first + 1 + np.random.permutation(np.repeat(np.arange(E - 1), -(-T // (E - 1)))[:T])) % E
    while np.bincount(second, minlength=E).max() != T // E:
        load = np.bincount(second, minlength=E); hi, lo = int(load.argmax()), int(load.argmin())
        t = np.flatnonzero((second == hi) & (first != lo))[0]; second[t] = lo
    slot_token = np.empty(E * C, np.int64); pos = np.empty((2, T), np.int64); fill = np.zeros(E, np.int64)
    place = np.stack([np.random.permutation(C) for _ in range(E)])
    for r, deal in enumerate((first, second)):
        for t in np.random.permutation(T):
            e = deal[t]; j = e * C + place[e, fill[e]]; fill[e] += 1; slot_token[j] = t; pos[r, t] = j
    g = np.random.uniform(0.2, 0.8, T)
    w_slot = np.empty(E * C); w_slot[pos[0]] = g; w_slot[pos[1]] = 1.0 - g
    w2 = [pack_weight(m, "e2m1") for m in n((E, N, H)) / np.sqrt(N) / s[None] * u[None, None, :]]
    w1 = [pack_weight(m, "e2m1") for m in n((E, H, K)) / np.sqrt(H) / u[None, :, None]]
    return {
        "dyT": (n((N, T)) * s).astype(np.float32),
        "a": n((H, E * C)).astype(np.float32),
        "w2_words": np.stack([m[0] for m in w2]),
        "w2_scales": np.stack([m[1] for m in w2]),
        "w1_words": np.stack([m[0] for m in w1]),
        "w1_scales": np.stack([m[1] for m in w1]),
        "gate": np.tile(w_slot, (N, 1)).astype(np.float32),
        "offs": striped(slot_token),
        "pos1": striped(pos[0]),
        "pos2": striped(pos[1]),
    }


def reference(dyT, a, w2_words, w2_scales, w1_words, w1_scales, gate, offs, pos1, pos2):
    idx = unstriped(offs)
    w2 = np.stack([unpack_weight(w2_words[e], w2_scales[e], "e2m1") for e in range(E)])
    w1 = np.stack([unpack_weight(w1_words[e], w1_scales[e], "e2m1") for e in range(E)])
    gq = mxq(f64(gate) * f64(dyT)[:, idx], 0, "e5m2")
    dh = by_expert(w2, gq)
    da = dh * d_relu(f64(a))
    dx = by_expert(w1, mxq(da, 0, "e5m2"))
    return dx[:, unstriped(pos1)] + dx[:, unstriped(pos2)]

@@ -1,0 +1,217 @@
+from contextlib import ExitStack
+
+import concourse.mybir as mybir
+
+N, H, K = 512, 512, 128
+T, E, C = 1024, 4, 512
+S = E * C
+P = 128
+PACK = 4
+
+FLOPS = 2 * S * (N * H + H * K)
+BYTES = 4 * N * T + 4 * H * S + E * (N * H + H * K) // 2 + E * (N * H + H * K) // 32 + 4 * S + 2 * P * (S + 2 * T) // 16 + 4 * K * T
+
+F32 = mybir.dt.float32
+BF16 = mybir.dt.bfloat16
+I32 = mybir.dt.int32
+U32 = mybir.dt.uint32
+U16 = mybir.dt.uint16
+U8 = mybir.dt.uint8
+E5M2X4 = mybir.dt.float8_e5m2_x4
+E2M1X4 = mybir.dt.float4_e2m1fn_x4
+MULT = mybir.AluOpType.mult
+IS_GT = mybir.AluOpType.is_gt
+
+
+def tile_moe_bdx_mlp_relu_kernel(
+    tc, dyT, a, w2_words, w2_scales, w1_words, w1_scales, gate, offs, pos1, pos2, out
+):
+    nc = tc.nc
+    with ExitStack() as ctx:
+        lists = ctx.enter_context(tc.tile_pool(name="lists", bufs=1))
+        held = ctx.enter_context(tc.tile_pool(name="held", bufs=1))
+        work = ctx.enter_context(tc.tile_pool(name="work", bufs=4))
+        dh_psum = ctx.enter_context(tc.psum_pool(name="dh_psum", bufs=6))
+        dx_psum = ctx.enter_context(tc.psum_pool(name="dx_psum", bufs=2))
+
+        offs_sb = lists.tile([P, S // 16], U16, name="offs_sb")
+        pos1_sb = lists.tile([P, T // 16], U16, name="pos1_sb")
+        pos2_sb = lists.tile([P, T // 16], U16, name="pos2_sb")
+
+        w2_raw = [held.tile([P, 2 * 2 * H], U8, name=f"w2_raw{h}", align_bytes=64) for h in range(2)]
+        w2_sb = [held.tile([P, 2 * 2 * H], U8, name=f"w2_sb{h}", align_bytes=64) for h in range(2)]
+        s2_raw = held.tile([P, E * H], U8, name="s2_raw", align_bytes=64)
+        s2_sb = [held.tile([P, 2 * H], U8, name=f"s2_sb{h}", align_bytes=64) for h in range(2)]
+        w1_sb = held.tile([P, E * 2 * K], U8, name="w1_sb", align_bytes=64)
+        s1_sb = held.tile([P, E * K], U8, name="s1_sb", align_bytes=64)
+        dy_sb = [held.tile([P, T], F32, name=f"dy_sb{t}") for t in range(PACK)]
+        gate_sb = [held.tile([P, C], F32, name=f"gate_sb{e}") for e in range(E)]
+        a_sb = [held.tile([P, PACK, C], F32, name=f"a_sb{e}") for e in range(E)]
+        dx_sb = held.tile([P, S], F32, name="dx_sb")
+
+        nc.gpsimd.memset(s2_raw[:].bitcast(I32), 0)
+        nc.gpsimd.memset(s1_sb[:].bitcast(I32), 0)
+
+        w2_i32 = w2_words.bitcast(I32)
+        w1_i32 = w1_words.bitcast(I32)
+        s2_i32 = w2_scales.bitcast(I32)
+        s1_i32 = w1_scales.bitcast(I32)
+        dy_planes = dyT.rearrange("(p t) c -> p t c", t=PACK)
+        a_planes = a.rearrange("(p t) c -> p t c", t=PACK)
+
+        def load_w2(h):
+            nc.sync.dma_start(
+                out=w2_raw[h][:].bitcast(I32).rearrange("p (e w) -> p e w", e=2),
+                in_=w2_i32[2 * h : 2 * h + 2, 0].rearrange("e p w -> p e w"),
+            )
+
+        def load_dy(t):
+            nc.sync.dma_start(out=dy_sb[t][:], in_=dy_planes[:, t, :])
+
+        def load_gate(e):
+            nc.sync.dma_start(out=gate_sb[e][:], in_=gate[0:P, e * C : (e + 1) * C])
+
+        def load_a(e):
+            nc.sync.dma_start(out=a_sb[e][:], in_=a_planes[:, :, e * C : (e + 1) * C])
+
+        load_w2(0)
+        nc.sync.dma_start(offs_sb[:], offs)
+        load_dy(0)
+        load_gate(0)
+        for q in range(4):
+            nc.scalar.dma_start(
+                out=s2_raw[32 * q : 32 * q + 4, :].bitcast(I32).rearrange("p (e w) -> p e w", e=E),
+                in_=s2_i32[:, 0, 4 * q : 4 * q + 4, :].rearrange("e f w -> f e w"),
+            )
+        load_dy(1)
+        load_dy(2)
+        load_dy(3)
+        load_gate(1)
+        load_gate(2)
+        load_w2(1)
+        load_a(0)
+        nc.sync.dma_start(
+            out=w1_sb[:].bitcast(I32).rearrange("p (e w) -> p e w", e=E), in_=w1_i32[:, 0].rearrange("e p w -> p e w")
+        )
+        for q in range(4):
+            nc.scalar.dma_start(
+                out=s1_sb[32 * q : 32 * q + 4, :].bitcast(I32).rearrange("p (e w) -> p e w", e=E),
+                in_=s1_i32[:, 0, 4 * q : 4 * q + 4, :].rearrange("e f w -> f e w"),
+            )
+        load_gate(3)
+        load_a(1)
+        load_a(2)
+        load_a(3)
+        nc.sync.dma_start(pos1_sb[:], pos1)
+        nc.sync.dma_start(pos2_sb[:], pos2)
+
+        def permute_w2(h):
+            nc.vector.tensor_copy(
+                out=w2_sb[h][:].bitcast(U16).rearrange("p (e t m) -> p e t m", e=2, t=PACK),
+                in_=w2_raw[h][:].bitcast(U16).rearrange("p (e m t) -> p e t m", e=2, t=PACK),
+            )
+            nc.vector.tensor_copy(
+                out=s2_sb[h][:].rearrange("p (e t m) -> p e t m", e=2, t=PACK),
+                in_=s2_raw[:, 2 * h * H : (2 * h + 2) * H].rearrange("p (e m t) -> p e t m", e=2, t=PACK),
+            )
+
+        def gather(e):
+            g4 = work.tile([P, PACK, C], F32, name="g4")
+            for t in range(PACK):
+                nc.vector.tensor_tensor(
+                    g4[:, t, :],
+                    dy_sb[t][:].indirect(offs_sb[:, e * (C // 16) : (e + 1) * (C // 16)]),
+                    gate_sb[e][:],
+                    MULT,
+                )
+            return g4
+
+        def interleave(src, name, lines):
+            flat = work.tile([P, C * PACK], BF16, name=name, align_bytes=64)
+            nc.scalar.copy(
+                flat[:].rearrange("p (c i t) -> p c t i", i=lines, t=PACK),
+                src[:].rearrange("p t (c i) -> p c t i", i=lines),
+            )
+            return flat
+
+        def quantise(flat, name):
+            codes = work.tile([P, C], U32, name=name + "_codes", align_bytes=64)
+            scales = work.tile([P, C], U8, name=name + "_scales", align_bytes=64)
+            nc.vector.quantize_mx(out=codes[:].bitcast(E5M2X4), scales=scales[:], in_=flat[:])
+            return codes, scales
+
+        def product2(e, g):
+            banks = []
+            for t in range(PACK):
+                dh = dh_psum.tile([P, C], F32, name="dh")
+                at = (e % 2) * H + t * P
+                nc.tensor.matmul_mx(
+                    out=dh[:],
+                    lhsT=w2_sb[e // 2][:, 2 * at : 2 * (at + P)].bitcast(E2M1X4),
+                    lhsT_scale=s2_sb[e // 2][:, at : at + P],
+                    rhs=g[0][:].bitcast(E5M2X4),
+                    rhs_scale=g[1][:],
+                    start=True,
+                    stop=True,
+                )
+                banks.append(dh)
+            return banks
+
+        def mask(e, banks):
+            da = work.tile([P, PACK, C], BF16, name="da")
+            for t in range(PACK):
+                nc.vector.scalar_tensor_tensor(
+                    out=da[:, t, :], in0=a_sb[e][:, t, :], scalar=0.0, in1=banks[t][:], op0=IS_GT, op1=MULT
+                )
+            return da
+
+        def product1(e, d):
+            dx = dx_psum.tile([P, C], F32, name="dx")
+            nc.tensor.matmul_mx(
+                out=dx[:],
+                lhsT=w1_sb[:, 2 * e * K : 2 * (e + 1) * K].bitcast(E2M1X4),
+                lhsT_scale=s1_sb[:, e * K : (e + 1) * K],
+                rhs=d[0][:].bitcast(E5M2X4),
+                rhs_scale=d[1][:],
+                start=True,
+                stop=True,
+            )
+            nc.scalar.copy(dx_sb[:, e * C : (e + 1) * C], dx[:])
+
+        permute_w2(0)
+        g4_0 = gather(0)
+        gi_0 = interleave(g4_0, "gi", 4)
+        g4_1 = gather(1)
+        gi_1 = interleave(g4_1, "gi", 4)
+        dh_0 = product2(0, quantise(gi_0, "g"))
+        g4_2 = gather(2)
+        gi_2 = interleave(g4_2, "gi", 4)
+        permute_w2(1)
+        dm_0 = mask(0, dh_0)
+        di_0 = interleave(dm_0, "di", 8)
+        dh_1 = product2(1, quantise(gi_1, "g"))
+        g4_3 = gather(3)
+        gi_3 = interleave(g4_3, "gi", 4)
+        dm_1 = mask(1, dh_1)
+        di_1 = interleave(dm_1, "di", 8)
+        dh_2 = product2(2, quantise(gi_2, "g"))
+        product1(0, quantise(di_0, "d"))
+        dm_2 = mask(2, dh_2)
+        di_2 = interleave(dm_2, "di", 8)
+        dh_3 = product2(3, quantise(gi_3, "g"))
+        product1(1, quantise(di_1, "d"))
+        dm_3 = mask(3, dh_3)
+        di_3 = interleave(dm_3, "di", 8)
+        product1(2, quantise(di_2, "d"))
+        product1(3, quantise(di_3, "d"))
+
+        half = T // 2
+        for h in range(2):
+            cols = slice(h * half // 16, (h + 1) * half // 16)
+            first = work.tile([P, half], F32, name="first")
+            second = work.tile([P, half], F32, name="second")
+            total = work.tile([P, half], F32, name="total")
+            nc.vector.tensor_copy(first[:], dx_sb[:].indirect(pos1_sb[:, cols]))
+            nc.vector.tensor_copy(second[:], dx_sb[:].indirect(pos2_sb[:, cols]))
+            nc.vector.tensor_add(total[:], first[:], second[:])
+            nc.sync.dma_start(out=out[:, h * half : (h + 1) * half], in_=total[:])

@@ -40,8 +40,8 @@ def tile_moe_bdx_mlp_relu_kernel(
 
         w2_raw = [held.tile([P, 2 * 2 * H], U8, name=f"w2_raw{h}", align_bytes=64) for h in range(2)]
         w2_sb = [held.tile([P, 2 * 2 * H], U8, name=f"w2_sb{h}", align_bytes=64) for h in range(2)]
-        s2_raw = held.tile([P, E * H], U8, name="s2_raw", align_bytes=64)
-        s2_sb = [held.tile([P, 2 * H], U8, name=f"s2_sb{h}", align_bytes=64) for h in range(2)]
+        s2_raw = held.tile([P, H], U8, name="s2_raw", align_bytes=64)
+        s2_sb = [held.tile([P, H], U8, name=f"s2_sb{e}", align_bytes=64) for e in range(E)]
         w1_sb = held.tile([P, E * 2 * K], U8, name="w1_sb", align_bytes=64)
         s1_sb = held.tile([P, E * K], U8, name="s1_sb", align_bytes=64)
         dy_sb = [held.tile([P, T], F32, name=f"dy_sb{t}") for t in range(PACK)]
@@ -51,6 +51,8 @@ def tile_moe_bdx_mlp_relu_kernel(
 
         nc.gpsimd.memset(s2_raw[:].bitcast(I32), 0)
         nc.gpsimd.memset(s1_sb[:].bitcast(I32), 0)
+        for e in range(1, E):
+            nc.gpsimd.memset(s2_sb[e][:].bitcast(I32), 0)
 
         w2_i32 = w2_words.bitcast(I32)
         w1_i32 = w1_words.bitcast(I32)
@@ -79,9 +81,8 @@ def tile_moe_bdx_mlp_relu_kernel(
         load_dy(0)
         load_gate(0)
         for q in range(4):
-            nc.scalar.dma_start(
-                out=s2_raw[32 * q : 32 * q + 4, :].bitcast(I32).rearrange("p (e w) -> p e w", e=E),
-                in_=s2_i32[:, 0, 4 * q : 4 * q + 4, :].rearrange("e f w -> f e w"),
+            nc.sync.dma_start(
+                out=s2_raw[32 * q : 32 * q + 16, :].bitcast(I32), in_=s2_i32[:, 0, 4 * q : 4 * q + 4, :]
             )
         load_dy(1)
         load_dy(2)
@@ -94,7 +95,7 @@ def tile_moe_bdx_mlp_relu_kernel(
             out=w1_sb[:].bitcast(I32).rearrange("p (e w) -> p e w", e=E), in_=w1_i32[:, 0].rearrange("e p w -> p e w")
         )
         for q in range(4):
-            nc.scalar.dma_start(
+            nc.sync.dma_start(
                 out=s1_sb[32 * q : 32 * q + 4, :].bitcast(I32).rearrange("p (e w) -> p e w", e=E),
                 in_=s1_i32[:, 0, 4 * q : 4 * q + 4, :].rearrange("e f w -> f e w"),
             )
@@ -110,10 +111,14 @@ def tile_moe_bdx_mlp_relu_kernel(
                 out=w2_sb[h][:].bitcast(U16).rearrange("p (e t m) -> p e t m", e=2, t=PACK),
                 in_=w2_raw[h][:].bitcast(U16).rearrange("p (e m t) -> p e t m", e=2, t=PACK),
             )
+
+        def permute_s2():
             nc.vector.tensor_copy(
-                out=s2_sb[h][:].rearrange("p (e t m) -> p e t m", e=2, t=PACK),
-                in_=s2_raw[:, 2 * h * H : (2 * h + 2) * H].rearrange("p (e m t) -> p e t m", e=2, t=PACK),
+                out=s2_sb[0][:].rearrange("p (t m) -> p t m", t=PACK),
+                in_=s2_raw[:].rearrange("p (m t) -> p t m", t=PACK),
             )
+            for e in range(1, E):
+                nc.sync.dma_start(out=s2_sb[e][0:112, :].bitcast(I32), in_=s2_sb[0][4 * e : 4 * e + 112, :].bitcast(I32))
 
         def gather(e):
             g4 = work.tile([P, PACK, C], F32, name="g4")
@@ -148,7 +153,7 @@ def tile_moe_bdx_mlp_relu_kernel(
                 nc.tensor.matmul_mx(
                     out=dh[:],
                     lhsT=w2_sb[e // 2][:, 2 * at : 2 * (at + P)].bitcast(E2M1X4),
-                    lhsT_scale=s2_sb[e // 2][:, at : at + P],
+                    lhsT_scale=s2_sb[e][:, t * P : (t + 1) * P],
                     rhs=g[0][:].bitcast(E5M2X4),
                     rhs_scale=g[1][:],
                     start=True,
@@ -180,6 +185,7 @@ def tile_moe_bdx_mlp_relu_kernel(
 
         permute_w2(0)
         g4_0 = gather(0)
+        permute_s2()
         gi_0 = interleave(g4_0, "gi", 4)
         g4_1 = gather(1)
         gi_1 = interleave(g4_1, "gi", 4)
@@ -188,30 +194,55 @@ def tile_moe_bdx_mlp_relu_kernel(
         gi_2 = interleave(g4_2, "gi", 4)
         permute_w2(1)
         dm_0 = mask(0, dh_0)
-        di_0 = interleave(dm_0, "di", 8)
+        di_0 = interleave(dm_0, "di", 4)
         dh_1 = product2(1, quantise(gi_1, "g"))
         g4_3 = gather(3)
         gi_3 = interleave(g4_3, "gi", 4)
         dm_1 = mask(1, dh_1)
-        di_1 = interleave(dm_1, "di", 8)
+        di_1 = interleave(dm_1, "di", 4)
         dh_2 = product2(2, quantise(gi_2, "g"))
         product1(0, quantise(di_0, "d"))
         dm_2 = mask(2, dh_2)
-        di_2 = interleave(dm_2, "di", 8)
+        di_2 = interleave(dm_2, "di", 4)
         dh_3 = product2(3, quantise(gi_3, "g"))
         product1(1, quantise(di_1, "d"))
-        dm_3 = mask(3, dh_3)
-        di_3 = interleave(dm_3, "di", 8)
+        da_3 = work.tile([P, PACK, C], BF16, name="da")
+        di_3 = work.tile([P, C * PACK], BF16, name="di", align_bytes=64)
+        d_3 = (
+            work.tile([P, C], U32, name="d_codes", align_bytes=64),
+            work.tile([P, C], U8, name="d_scales", align_bytes=64),
+        )
+        parts = 2
+        wide = C // parts
+        for j in range(parts):
+            part = slice(j * wide, (j + 1) * wide)
+            for t in range(PACK):
+                nc.vector.scalar_tensor_tensor(
+                    out=da_3[:, t, part], in0=a_sb[3][:, t, part], scalar=0.0, in1=dh_3[t][:, part], op0=IS_GT, op1=MULT
+                )
+            nc.scalar.copy(
+                di_3[:, PACK * j * wide : PACK * (j + 1) * wide].rearrange("p (c i t) -> p c t i", i=4, t=PACK),
+                da_3[:, :, part].rearrange("p t (c i) -> p c t i", i=4),
+            )
         product1(2, quantise(di_2, "d"))
-        product1(3, quantise(di_3, "d"))
+        for j in range(parts):
+            part = slice(j * wide, (j + 1) * wide)
+            nc.vector.quantize_mx(
+                out=d_3[0][:, part].bitcast(E5M2X4),
+                scales=d_3[1][:, part],
+                in_=di_3[:, PACK * j * wide : PACK * (j + 1) * wide],
+            )
+        product1(3, d_3)
 
         half = T // 2
+        first = held.tile([P, T], F32, name="first")
+        nc.vector.tensor_copy(first[:], dx_sb[:].indirect(pos1_sb[:]))
+        second = [work.tile([P, half], F32, name="second") for h in range(2)]
         for h in range(2):
-            cols = slice(h * half // 16, (h + 1) * half // 16)
-            first = work.tile([P, half], F32, name="first")
-            second = work.tile([P, half], F32, name="second")
+            nc.vector.tensor_copy(
+                second[h][:], dx_sb[:].indirect(pos2_sb[:, h * half // 16 : (h + 1) * half // 16])
+            )
+        for h in range(2):
             total = work.tile([P, half], F32, name="total")
-            nc.vector.tensor_copy(first[:], dx_sb[:].indirect(pos1_sb[:, cols]))
-            nc.vector.tensor_copy(second[:], dx_sb[:].indirect(pos2_sb[:, cols]))
-            nc.vector.tensor_add(total[:], first[:], second[:])
+            nc.vector.tensor_add(total[:], first[:, h * half : (h + 1) * half], second[h][:])
             nc.sync.dma_start(out=out[:, h * half : (h + 1) * half], in_=total[:])

@@ -80,17 +80,17 @@ def tile_moe_bdx_mlp_relu_kernel(
         nc.sync.dma_start(offs_sb[:], offs)
         load_dy(0)
         load_gate(0)
-        for q in range(4):
-            nc.sync.dma_start(
-                out=s2_raw[32 * q : 32 * q + 16, :].bitcast(I32), in_=s2_i32[:, 0, 4 * q : 4 * q + 4, :]
-            )
         load_dy(1)
         load_dy(2)
         load_dy(3)
         load_gate(1)
+        for q in range(4):
+            nc.sync.dma_start(
+                out=s2_raw[32 * q : 32 * q + 16, :].bitcast(I32), in_=s2_i32[:, 0, 4 * q : 4 * q + 4, :]
+            )
+        load_a(0)
         load_gate(2)
         load_w2(1)
-        load_a(0)
         nc.sync.dma_start(
             out=w1_sb[:].bitcast(I32).rearrange("p (e w) -> p e w", e=E), in_=w1_i32[:, 0].rearrange("e p w -> p e w")
         )
@@ -185,10 +185,10 @@ def tile_moe_bdx_mlp_relu_kernel(
 
         permute_w2(0)
         g4_0 = gather(0)
-        permute_s2()
         gi_0 = interleave(g4_0, "gi", 4)
         g4_1 = gather(1)
         gi_1 = interleave(g4_1, "gi", 4)
+        permute_s2()
         dh_0 = product2(0, quantise(gi_0, "g"))
         g4_2 = gather(2)
         gi_2 = interleave(g4_2, "gi", 4)
@@ -202,10 +202,9 @@ def tile_moe_bdx_mlp_relu_kernel(
         di_1 = interleave(dm_1, "di", 4)
         dh_2 = product2(2, quantise(gi_2, "g"))
         product1(0, quantise(di_0, "d"))
+        dh_3 = product2(3, quantise(gi_3, "g"))
         dm_2 = mask(2, dh_2)
         di_2 = interleave(dm_2, "di", 4)
-        dh_3 = product2(3, quantise(gi_3, "g"))
-        product1(1, quantise(di_1, "d"))
         da_3 = work.tile([P, PACK, C], BF16, name="da")
         di_3 = work.tile([P, C * PACK], BF16, name="di", align_bytes=64)
         d_3 = (
@@ -224,6 +223,7 @@ def tile_moe_bdx_mlp_relu_kernel(
                 di_3[:, PACK * j * wide : PACK * (j + 1) * wide].rearrange("p (c i t) -> p c t i", i=4, t=PACK),
                 da_3[:, :, part].rearrange("p t (c i) -> p c t i", i=4),
             )
+        product1(1, quantise(di_1, "d"))
         product1(2, quantise(di_2, "d"))
         for j in range(parts):
             part = slice(j * wide, (j + 1) * wide)
@@ -244,5 +244,6 @@ def tile_moe_bdx_mlp_relu_kernel(
             )
         for h in range(2):
             total = work.tile([P, half], F32, name="total")
-            nc.vector.tensor_add(total[:], first[:, h * half : (h + 1) * half], second[h][:])
+            adder = nc.gpsimd if h == 0 else nc.vector
+            adder.tensor_tensor(total[:], first[:, h * half : (h + 1) * half], second[h][:], mybir.AluOpType.add)
             nc.sync.dma_start(out=out[:, h * half : (h + 1) * half], in_=total[:])

from contextlib import ExitStack

import concourse.mybir as mybir

N, H, K = 512, 512, 128
T, E, C = 1024, 4, 512
S = E * C
P = 128
PACK = 4

FLOPS = 2 * S * (N * H + H * K)
BYTES = 4 * N * T + 4 * H * S + E * (N * H + H * K) // 2 + E * (N * H + H * K) // 32 + 4 * S + 2 * P * (S + 2 * T) // 16 + 4 * K * T

F32 = mybir.dt.float32
BF16 = mybir.dt.bfloat16
I32 = mybir.dt.int32
U32 = mybir.dt.uint32
U16 = mybir.dt.uint16
U8 = mybir.dt.uint8
E5M2X4 = mybir.dt.float8_e5m2_x4
E2M1X4 = mybir.dt.float4_e2m1fn_x4
MULT = mybir.AluOpType.mult
IS_GT = mybir.AluOpType.is_gt


def tile_moe_bdx_mlp_relu_kernel(
    tc, dyT, a, w2_words, w2_scales, w1_words, w1_scales, gate, offs, pos1, pos2, out
):
    nc = tc.nc
    with ExitStack() as ctx:
        lists = ctx.enter_context(tc.tile_pool(name="lists", bufs=1))
        held = ctx.enter_context(tc.tile_pool(name="held", bufs=1))
        work = ctx.enter_context(tc.tile_pool(name="work", bufs=4))
        dh_psum = ctx.enter_context(tc.psum_pool(name="dh_psum", bufs=6))
        dx_psum = ctx.enter_context(tc.psum_pool(name="dx_psum", bufs=2))

        offs_sb = lists.tile([P, S // 16], U16, name="offs_sb")
        pos1_sb = lists.tile([P, T // 16], U16, name="pos1_sb")
        pos2_sb = lists.tile([P, T // 16], U16, name="pos2_sb")

        w2_raw = [held.tile([P, 2 * 2 * H], U8, name=f"w2_raw{h}", align_bytes=64) for h in range(2)]
        w2_sb = [held.tile([P, 2 * 2 * H], U8, name=f"w2_sb{h}", align_bytes=64) for h in range(2)]
        s2_raw = held.tile([P, H], U8, name="s2_raw", align_bytes=64)
        s2_sb = [held.tile([P, H], U8, name=f"s2_sb{e}", align_bytes=64) for e in range(E)]
        w1_sb = held.tile([P, E * 2 * K], U8, name="w1_sb", align_bytes=64)
        s1_sb = held.tile([P, E * K], U8, name="s1_sb", align_bytes=64)
        dy_sb = [held.tile([P, T], F32, name=f"dy_sb{t}") for t in range(PACK)]
        gate_sb = [held.tile([P, C], F32, name=f"gate_sb{e}") for e in range(E)]
        a_sb = [held.tile([P, PACK, C], F32, name=f"a_sb{e}") for e in range(E)]
        dx_sb = held.tile([P, S], F32, name="dx_sb")

        nc.gpsimd.memset(s2_raw[:].bitcast(I32), 0)
        nc.gpsimd.memset(s1_sb[:].bitcast(I32), 0)
        for e in range(1, E):
            nc.gpsimd.memset(s2_sb[e][:].bitcast(I32), 0)

        w2_i32 = w2_words.bitcast(I32)
        w1_i32 = w1_words.bitcast(I32)
        s2_i32 = w2_scales.bitcast(I32)
        s1_i32 = w1_scales.bitcast(I32)
        dy_planes = dyT.rearrange("(p t) c -> p t c", t=PACK)
        a_planes = a.rearrange("(p t) c -> p t c", t=PACK)

        def load_w2(h):
            nc.sync.dma_start(
                out=w2_raw[h][:].bitcast(I32).rearrange("p (e w) -> p e w", e=2),
                in_=w2_i32[2 * h : 2 * h + 2, 0].rearrange("e p w -> p e w"),
            )

        def load_dy(t):
            nc.sync.dma_start(out=dy_sb[t][:], in_=dy_planes[:, t, :])

        def load_gate(e):
            nc.sync.dma_start(out=gate_sb[e][:], in_=gate[0:P, e * C : (e + 1) * C])

        def load_a(e):
            nc.sync.dma_start(out=a_sb[e][:], in_=a_planes[:, :, e * C : (e + 1) * C])

        load_w2(0)
        nc.sync.dma_start(offs_sb[:], offs)
        load_dy(0)
        load_gate(0)
        load_dy(1)
        load_dy(2)
        load_dy(3)
        load_gate(1)
        for q in range(4):
            nc.sync.dma_start(
                out=s2_raw[32 * q : 32 * q + 16, :].bitcast(I32), in_=s2_i32[:, 0, 4 * q : 4 * q + 4, :]
            )
        load_a(0)
        load_gate(2)
        load_w2(1)
        nc.sync.dma_start(
            out=w1_sb[:].bitcast(I32).rearrange("p (e w) -> p e w", e=E), in_=w1_i32[:, 0].rearrange("e p w -> p e w")
        )
        for q in range(4):
            nc.sync.dma_start(
                out=s1_sb[32 * q : 32 * q + 4, :].bitcast(I32).rearrange("p (e w) -> p e w", e=E),
                in_=s1_i32[:, 0, 4 * q : 4 * q + 4, :].rearrange("e f w -> f e w"),
            )
        load_gate(3)
        load_a(1)
        load_a(2)
        load_a(3)
        nc.sync.dma_start(pos1_sb[:], pos1)
        nc.sync.dma_start(pos2_sb[:], pos2)

        def permute_w2(h):
            nc.vector.tensor_copy(
                out=w2_sb[h][:].bitcast(U16).rearrange("p (e t m) -> p e t m", e=2, t=PACK),
                in_=w2_raw[h][:].bitcast(U16).rearrange("p (e m t) -> p e t m", e=2, t=PACK),
            )

        def permute_s2():
            nc.vector.tensor_copy(
                out=s2_sb[0][:].rearrange("p (t m) -> p t m", t=PACK),
                in_=s2_raw[:].rearrange("p (m t) -> p t m", t=PACK),
            )
            for e in range(1, E):
                nc.sync.dma_start(out=s2_sb[e][0:112, :].bitcast(I32), in_=s2_sb[0][4 * e : 4 * e + 112, :].bitcast(I32))

        def gather(e):
            g4 = work.tile([P, PACK, C], F32, name="g4")
            for t in range(PACK):
                nc.vector.tensor_tensor(
                    g4[:, t, :],
                    dy_sb[t][:].indirect(offs_sb[:, e * (C // 16) : (e + 1) * (C // 16)]),
                    gate_sb[e][:],
                    MULT,
                )
            return g4

        def interleave(src, name, lines):
            flat = work.tile([P, C * PACK], BF16, name=name, align_bytes=64)
            nc.scalar.copy(
                flat[:].rearrange("p (c i t) -> p c t i", i=lines, t=PACK),
                src[:].rearrange("p t (c i) -> p c t i", i=lines),
            )
            return flat

        def quantise(flat, name):
            codes = work.tile([P, C], U32, name=name + "_codes", align_bytes=64)
            scales = work.tile([P, C], U8, name=name + "_scales", align_bytes=64)
            nc.vector.quantize_mx(out=codes[:].bitcast(E5M2X4), scales=scales[:], in_=flat[:])
            return codes, scales

        def product2(e, g):
            banks = []
            for t in range(PACK):
                dh = dh_psum.tile([P, C], F32, name="dh")
                at = (e % 2) * H + t * P
                nc.tensor.matmul_mx(
                    out=dh[:],
                    lhsT=w2_sb[e // 2][:, 2 * at : 2 * (at + P)].bitcast(E2M1X4),
                    lhsT_scale=s2_sb[e][:, t * P : (t + 1) * P],
                    rhs=g[0][:].bitcast(E5M2X4),
                    rhs_scale=g[1][:],
                    start=True,
                    stop=True,
                )
                banks.append(dh)
            return banks

        def mask(e, banks):
            da = work.tile([P, PACK, C], BF16, name="da")
            for t in range(PACK):
                nc.vector.scalar_tensor_tensor(
                    out=da[:, t, :], in0=a_sb[e][:, t, :], scalar=0.0, in1=banks[t][:], op0=IS_GT, op1=MULT
                )
            return da

        def product1(e, d):
            dx = dx_psum.tile([P, C], F32, name="dx")
            nc.tensor.matmul_mx(
                out=dx[:],
                lhsT=w1_sb[:, 2 * e * K : 2 * (e + 1) * K].bitcast(E2M1X4),
                lhsT_scale=s1_sb[:, e * K : (e + 1) * K],
                rhs=d[0][:].bitcast(E5M2X4),
                rhs_scale=d[1][:],
                start=True,
                stop=True,
            )
            nc.scalar.copy(dx_sb[:, e * C : (e + 1) * C], dx[:])

        permute_w2(0)
        g4_0 = gather(0)
        gi_0 = interleave(g4_0, "gi", 4)
        g4_1 = gather(1)
        gi_1 = interleave(g4_1, "gi", 4)
        permute_s2()
        dh_0 = product2(0, quantise(gi_0, "g"))
        g4_2 = gather(2)
        gi_2 = interleave(g4_2, "gi", 4)
        permute_w2(1)
        dm_0 = mask(0, dh_0)
        di_0 = interleave(dm_0, "di", 4)
        dh_1 = product2(1, quantise(gi_1, "g"))
        g4_3 = gather(3)
        gi_3 = interleave(g4_3, "gi", 4)
        dm_1 = mask(1, dh_1)
        di_1 = interleave(dm_1, "di", 4)
        dh_2 = product2(2, quantise(gi_2, "g"))
        product1(0, quantise(di_0, "d"))
        dh_3 = product2(3, quantise(gi_3, "g"))
        dm_2 = mask(2, dh_2)
        di_2 = interleave(dm_2, "di", 4)
        da_3 = work.tile([P, PACK, C], BF16, name="da")
        di_3 = work.tile([P, C * PACK], BF16, name="di", align_bytes=64)
        d_3 = (
            work.tile([P, C], U32, name="d_codes", align_bytes=64),
            work.tile([P, C], U8, name="d_scales", align_bytes=64),
        )
        parts = 2
        wide = C // parts
        for j in range(parts):
            part = slice(j * wide, (j + 1) * wide)
            for t in range(PACK):
                nc.vector.scalar_tensor_tensor(
                    out=da_3[:, t, part], in0=a_sb[3][:, t, part], scalar=0.0, in1=dh_3[t][:, part], op0=IS_GT, op1=MULT
                )
            nc.scalar.copy(
                di_3[:, PACK * j * wide : PACK * (j + 1) * wide].rearrange("p (c i t) -> p c t i", i=4, t=PACK),
                da_3[:, :, part].rearrange("p t (c i) -> p c t i", i=4),
            )
        product1(1, quantise(di_1, "d"))
        product1(2, quantise(di_2, "d"))
        for j in range(parts):
            part = slice(j * wide, (j + 1) * wide)
            nc.vector.quantize_mx(
                out=d_3[0][:, part].bitcast(E5M2X4),
                scales=d_3[1][:, part],
                in_=di_3[:, PACK * j * wide : PACK * (j + 1) * wide],
            )
        product1(3, d_3)

        half = T // 2
        first = held.tile([P, T], F32, name="first")
        nc.vector.tensor_copy(first[:], dx_sb[:].indirect(pos1_sb[:]))
        second = [work.tile([P, half], F32, name="second") for h in range(2)]
        for h in range(2):
            nc.vector.tensor_copy(
                second[h][:], dx_sb[:].indirect(pos2_sb[:, h * half // 16 : (h + 1) * half // 16])
            )
        for h in range(2):
            total = work.tile([P, half], F32, name="total")
            adder = nc.gpsimd if h == 0 else nc.vector
            adder.tensor_tensor(total[:], first[:, h * half : (h + 1) * half], second[h][:], mybir.AluOpType.add)
            nc.sync.dma_start(out=out[:, h * half : (h + 1) * half], in_=total[:])
